import numpy as np
import ml_dtypes


def mxq(x, axis, fmt="e4m3"):
    dtype, down = {"e4m3": (ml_dtypes.float8_e4m3fn, 7), "e5m2": (ml_dtypes.float8_e5m2, 14)}[fmt]
    v = np.moveaxis(np.asarray(x, np.float32).astype(ml_dtypes.bfloat16).astype(np.float64), axis, -1)
    blocks = v.reshape(v.shape[:-1] + (-1, 32))
    amax = np.abs(blocks).max(-1, keepdims=True)
    byte = np.maximum(np.where(amax > 0, np.frexp(amax)[1] - 1 + 127, 0) - down, 1)
    scale = np.exp2(byte - 127.0)
    codes = (blocks / scale).astype(np.float32).astype(dtype).astype(np.float64)
    return np.moveaxis((codes * scale).reshape(v.shape), -1, axis)


WIDE = False


def mx_kscale(k):
    if not WIDE:
        return np.ones(k)
    levels = np.array([10, -10, 5, -5, 0])
    if k % 512:
        return np.exp2(np.random.permutation(np.resize(levels, k // 32))).repeat(32)
    a = np.empty((k // 512, 16))
    for p in range(k // 512):
        a[p, :8] = np.random.permutation(np.resize(levels, 8))
        for g in range(8):
            far = levels[np.abs(levels - a[p, g]) >= 10]
            a[p, g + 8] = far[np.random.randint(len(far))]
    return np.exp2(a.ravel()).repeat(32)


def f64(x):
    return np.asarray(x).astype(np.float64)


def striped(idx):
    return np.tile(idx.reshape(-1, 16).T, (8, 1)).astype(np.uint16)


def unstriped(offs):
    return offs[:16].T.reshape(-1).astype(np.int64)


E2M1 = np.array([0.0, 0.5, 1.0, 1.5, 2.0, 3.0, 4.0, 6.0, -0.0, -0.5, -1.0, -1.5, -2.0, -3.0, -4.0, -6.0])


def pack_weight(w, fmt):
    k, n = w.shape
    w = f64(np.asarray(w, np.float32).astype(ml_dtypes.bfloat16)).reshape(k // 32, 32, n)
    amax = np.abs(w).max(1)
    if fmt == "e4m3":
        byte = np.frexp(amax)[1] - 1 + 127 - 7
    else:
        mant, ex = np.frexp(amax / 6.0)
        byte = np.where(mant > 0.5, ex, ex - 1) + 127
    byte = np.clip(np.where(amax > 0, byte, 1), 1, 254)
    scaled = (w * np.exp2(127.0 - byte)[:, None, :]).reshape(k, n).astype(np.float32)
    by_word = np.ascontiguousarray(scaled.reshape(k // 512, 128, 4, n).transpose(0, 1, 3, 2))
    if fmt == "e4m3":
        words = by_word.astype(ml_dtypes.float8_e4m3fn).view(np.uint8)
    else:
        c = by_word.astype(ml_dtypes.float4_e2m1fn).view(np.uint8) & 0xF
        words = (c[..., 0::2] | (c[..., 1::2] << 4)).reshape(k // 512, 128, 2 * n)
    return np.ascontiguousarray(words), np.ascontiguousarray(byte.astype(np.uint8).reshape(k // 512, 16, n))


def unpack_weight(words, scales, fmt):
    g, _, n = scales.shape
    words = np.ascontiguousarray(words).reshape(g, 128, n, -1)
    if fmt == "e4m3":
        vals = words.view(ml_dtypes.float8_e4m3fn).astype(np.float64)
    else:
        nib = np.empty((g, 128, n, 4), np.uint8)
        nib[..., 0::2] = words & 0xF
        nib[..., 1::2] = words >> 4
        vals = E2M1[nib]
    vals = vals * np.repeat(np.exp2(scales.astype(np.float64) - 127.0), 8, axis=1)[..., None]
    return vals.transpose(0, 1, 3, 2).reshape(g * 512, n)


def gelu(v):
    return 0.5 * v * (1.0 + np.tanh(np.sqrt(2.0 / np.pi) * (v + 0.044715 * v**3)))


K, T, S, S2 = 1024, 2048, 512, 1024

def setup_inputs():
    n = np.random.standard_normal
    s = mx_kscale(K)[:, None]
    d = {}
    d["tab_words"], d["tab_scales"] = pack_weight(n((K, T)) * s, "e4m3")
    d["offs"] = striped(np.random.permutation(T)[:S])
    d["offs2"] = striped(np.random.permutation(T)[:S2])
    d["w1"] = (n((K, K)) / (s * s.T * K)).astype(np.float32)
    d["w4_words"], d["w4_scales"] = pack_weight(n((K, K)) / (s * s.T * K), "e2m1")
    d["wgt"] = np.exp(0.5 * n(S2)).astype(np.float32)
    return d

def reference(tab_words, tab_scales, offs, offs2, w1, w4_words, w4_scales, wgt):
    TW = unpack_weight(tab_words, tab_scales, "e4m3")
    v = TW[:, unstriped(offs)]
    v2 = TW[:, unstriped(offs2)]
    w4 = unpack_weight(w4_words, w4_scales, "e2m1")
    h1 = np.abs(mxq(f64(w1), 0, "e4m3").T @ v)
    h2 = np.abs(w4.T @ v)
    e1 = v2.T @ mxq(h1, 0, "e4m3")
    e2 = v2.T @ mxq(h2, 0, "e4m3")
    total = np.square(e1) + f64(wgt)[:, None] * np.square(e2)
    return np.sqrt(total)

@@ -1,0 +1,305 @@
+from contextlib import ExitStack
+
+import concourse.mybir as mybir
+from concourse.masks import make_identity
+
+K, T, S, S2 = 1024, 2048, 512, 1024
+FLOPS = 2 * (2 * K * K * S + 2 * K * S2 * S)
+
+F32 = mybir.dt.float32
+BF16 = mybir.dt.bfloat16
+I32 = mybir.dt.int32
+U32 = mybir.dt.uint32
+U16 = mybir.dt.uint16
+U8 = mybir.dt.uint8
+FP8X4 = mybir.dt.float8_e4m3fn_x4
+FP4X4 = mybir.dt.float4_e2m1fn_x4
+ACT = mybir.ActivationFunctionType
+ALU = mybir.AluOpType
+
+P = 128
+PACK = 4
+KP = P * PACK
+PASSES = K // KP
+JC = 128
+HALF = S2 // 2
+CAST_ON_SCALAR = [2]
+SQUARE_ON_VECTOR = []
+WEIGHTED_ON_VECTOR = [4,5,6]
+PLACES = {"w4_w0":0,"v2_w00":0,"w4_s0":2048,"v2_s0":2048,"h2_bf0":4096,"w1_bf01":4096,"h1_bf0":8192,"v2_s1":8192,"v2_w10":8704,"h1_bf1":12288,"v2_w11":12288}
+
+
+def tile_list_depot_hazard_magnitude_kernel(
+    tc, tab_words, tab_scales, offs, offs2, w1, w4_words, w4_scales, wgt, out
+):
+    nc = tc.nc
+    with ExitStack() as ctx:
+        keep = ctx.enter_context(tc.tile_pool(name="keep", bufs=1))
+        stage = ctx.enter_context(tc.tile_pool(name="stage", bufs=1))
+        ring = ctx.enter_context(tc.tile_pool(name="ring", bufs=4))
+        psum = ctx.enter_context(tc.psum_pool(name="psum", bufs=4))
+
+        def held(shape, dtype, name):
+            if name in PLACES:
+                return stage.tile(shape, dtype, name=name, align_bytes=64, offset=PLACES[name])
+            return keep.tile(shape, dtype, name=name, align_bytes=64)
+
+        idx = keep.tile([P, S // 16], U16, name="idx")
+        idx2 = keep.tile([P, S2 // 16], U16, name="idx2")
+        tab_w = [held([P, T], I32, "tab_w%d" % a) for a in range(PASSES)]
+        tab_s = held([P, T], U8, "tab_s")
+        w4_raw = held([P, PASSES, 2 * K], U8, "w4_raw")
+        w4s_raw = held([P, PASSES, K], U8, "w4s_raw")
+        v_s_low = held([P, S], U8, "v_s_low")
+        wgt_rows = held([S2 // P, P], F32, "wgt_rows")
+        root_rows = held([P, P], F32, "root_rows")
+        ident = held([P, P], F32, "ident")
+        root_w = held([P, S2 // P], F32, "root_w")
+
+        nc.gpsimd.memset(tab_s[:].bitcast(I32), 0)
+        make_identity(nc, ident[:])
+        nc.vector.memset(w4s_raw[:].rearrange("p a n -> p (a n)").bitcast(I32), 0)
+        nc.vector.memset(root_rows[:], 0.0)
+        nc.vector.memset(v_s_low[:].bitcast(I32), 0)
+
+        def load_table(a):
+            nc.sync.dma_start(out=tab_w[a][:], in_=tab_words[a].rearrange("p t i -> p (t i)").bitcast(I32))
+
+        nc.sync.dma_start(idx[:], offs)
+        nc.sync.dma_start(out=wgt_rows[:], in_=wgt.rearrange("(c p) -> c p", p=P))
+        for q in range(4):
+            nc.sync.dma_start(
+                out=tab_s[32 * q : 32 * q + 8, :].bitcast(I32),
+                in_=tab_scales[:, 4 * q : 4 * q + 4, :].bitcast(I32),
+            )
+        nc.sync.dma_start(out=w4_raw[:].bitcast(I32), in_=w4_words.rearrange("a p n -> p a n").bitcast(I32))
+        load_table(0)
+        for q in range(4):
+            nc.sync.dma_start(
+                out=w4s_raw[32 * q : 32 * q + 4, :, :].bitcast(I32),
+                in_=w4_scales[:, 4 * q : 4 * q + 4, :].rearrange("a r n -> r a n").bitcast(I32),
+            )
+        load_table(1)
+        nc.sync.dma_start(idx2[:], offs2)
+        w1_raw = {}
+        for b in range(PASSES):
+            for a in range(PASSES):
+                w1_raw[a, b] = held([P, PACK, KP], F32, "w1_raw%d%d" % (a, b))
+                nc.sync.dma_start(
+                    out=w1_raw[a, b][:],
+                    in_=w1[KP * a : KP * (a + 1), KP * b : KP * (b + 1)].rearrange("(p i) c -> p i c", i=PACK),
+                )
+
+        nc.scalar.activation(root_rows[0 : S2 // P, :], wgt_rows[:], ACT.Sqrt)
+        root_cols = psum.tile([P, KP], F32, name="bank")
+        nc.tensor.transpose(root_cols[:, 0:P], root_rows[:], ident[:])
+        nc.scalar.copy(root_w[:], root_cols[:, 0 : S2 // P])
+
+        def gather_words(dst, a, offsets):
+            nc.vector.tensor_copy(dst, tab_w[a][:].bitcast(U32).indirect(offsets))
+
+        def gather_scales(dst, offsets):
+            nc.vector.tensor_copy(dst, tab_s[:].indirect(offsets))
+
+        w4_w = {}
+        w4_s = {}
+
+        def deal_w4_scales(b):
+            w4_s[b] = held([P, PASSES * KP], U8, "w4_s%d" % b)
+            nc.vector.tensor_copy(
+                w4_s[b][:].rearrange("p (a t q) -> p a t q", a=PASSES, t=PACK),
+                w4s_raw[:, :, KP * b : KP * (b + 1)].rearrange("p a (q t) -> p a t q", t=PACK),
+            )
+
+        def deal_w4_words(b):
+            w4_w[b] = held([P, PASSES * K], U8, "w4_w%d" % b)
+            nc.vector.tensor_copy(
+                w4_w[b][:].bitcast(U16).rearrange("p (a t q) -> p a t q", a=PASSES, t=PACK),
+                w4_raw[:, :, K * b : K * (b + 1)].bitcast(U16).rearrange("p a (q t) -> p a t q", t=PACK),
+            )
+
+        v_s = held([P, S], U8, "v_s")
+        v_w = [held([P, S], U32, "v_w%d" % a) for a in range(PASSES)]
+        gather_scales(v_s[:], idx[:])
+        nc.scalar.dma_start(out=v_s_low[0 : P - 4, :].bitcast(I32), in_=v_s[4:P, :].bitcast(I32))
+        deal_w4_words(0)
+        deal_w4_words(1)
+        gather_words(v_w[0][:], 0, idx[:])
+        deal_w4_scales(0)
+        for half in range(2):
+            gather_words(v_w[1][:, 256 * half : 256 * (half + 1)], 1, idx[:, 16 * half : 16 * (half + 1)])
+        deal_w4_scales(1)
+
+        h_bf = {}
+
+        def first_products(name, b, stationary, v_scales):
+            h_bf[name, b] = held([P, PACK * S], BF16, "%s_bf%d" % (name, b))
+            for jc in range(S // JC):
+                cols = slice(JC * jc, JC * (jc + 1))
+                bank = psum.tile([P, KP], F32, name="h_bank")
+                for a in range(PASSES):
+                    for t in range(PACK):
+                        codes, scales = stationary(a, t)
+                        nc.tensor.matmul_mx(
+                            out=bank[:, JC * t : JC * (t + 1)],
+                            lhsT=codes,
+                            lhsT_scale=scales,
+                            rhs=v_w[a][:, cols].bitcast(FP8X4),
+                            rhs_scale=v_scales[a][:, cols],
+                            start=(a == 0 and t == 0),
+                            stop=(a == PASSES - 1 and t == PACK - 1),
+                        )
+                nc.scalar.activation(
+                    h_bf[name, b][:, KP * jc : KP * (jc + 1)].rearrange("p (j t) -> p j t", t=PACK),
+                    bank[:].rearrange("p (t j) -> p j t", t=PACK),
+                    ACT.Abs,
+                )
+
+        def quantize(name, values):
+            codes = held([P, KP], U32, name + "_w")
+            scales = held([P, KP], U8, name + "_s")
+            nc.vector.quantize_mx(out=codes[:].bitcast(FP8X4), scales=scales[:], in_=values[:])
+            return codes, scales
+
+        def h2_block(b):
+            def stationary(a, t):
+                c = P * (PACK * a + t)
+                return w4_w[b][:, 2 * c : 2 * (c + P)].bitcast(FP4X4), w4_s[b][:, c : c + P]
+
+            first_products("h2", b, stationary, [v_s[:], v_s_low[:]])
+
+        w1_bf = {}
+        w1_q = {}
+
+        def cast_w1(a, b):
+            w1_bf[a, b] = held([P, PACK * KP], BF16, "w1_bf%d%d" % (a, b))
+            dst = w1_bf[a, b][:].rearrange("p (t q i) -> p q t i", t=PACK, i=PACK)
+            src = w1_raw[a, b][:].rearrange("p i (q t) -> p q t i", t=PACK)
+            if PASSES * b + a in CAST_ON_SCALAR:
+                nc.scalar.copy(dst, src)
+            else:
+                nc.vector.tensor_copy(dst, src)
+
+        def quantize_w1(a, b):
+            w1_q[a, b] = quantize("w1_q%d%d" % (a, b), w1_bf[a, b])
+
+        def h1_block(b):
+            def stationary(a, t):
+                codes, scales = w1_q[a, b]
+                return codes[:, P * t : P * (t + 1)].bitcast(FP8X4), scales[:, P * t : P * (t + 1)]
+
+            first_products("h1", b, stationary, [v_s[:], v_s[4:P, :]])
+
+        h1_q = {}
+        h2_q = {}
+
+        def quantize_h(store, name, b):
+            store[b] = quantize("%s_q%d" % (name, b), h_bf[name, b])
+
+        v2_w = {}
+        v2_s = {}
+
+        def stored_offsets(half):
+            return idx2[:, HALF // 16 * half : HALF // 16 * (half + 1)]
+
+        def gather_stored_scales(half):
+            v2_s[half] = held([P, HALF], U8, "v2_s%d" % half)
+            gather_scales(v2_s[half][:], stored_offsets(half))
+
+        def gather_stored_words(half, b):
+            v2_w[half, b] = held([P, HALF], U32, "v2_w%d%d" % (half, b))
+            gather_words(v2_w[half, b][:], b, stored_offsets(half))
+
+        def second_product(c, h_q, bank_name):
+            half, cols = divmod(P * c, HALF)
+            bank = psum.tile([P, S], F32, name=bank_name)
+            for b in range(PASSES):
+                nc.tensor.matmul_mx(
+                    out=bank[:],
+                    lhsT=v2_w[half, b][:, cols : cols + P].bitcast(FP8X4),
+                    lhsT_scale=v2_s[half][4 * b : P, cols : cols + P],
+                    rhs=h_q[b][0][:].bitcast(FP8X4),
+                    rhs_scale=h_q[b][1][:],
+                    start=(b == 0),
+                    stop=(b == PASSES - 1),
+                )
+            return bank
+
+        sq2 = {}
+
+        def weighted_square(c):
+            bank = second_product(c, h2_q, "bank" if c < 4 else "h_bank")
+            sq2[c] = held([P, S], F32, "sq2_%d" % c)
+            if c in WEIGHTED_ON_VECTOR:
+                scaled = held([P, S], F32, "scaled%d" % c)
+                nc.vector.tensor_scalar(scaled[:], bank[:], root_w[:, c : c + 1], None, ALU.mult)
+                nc.vector.tensor_tensor(sq2[c][:], scaled[:], scaled[:], ALU.mult)
+            else:
+                nc.scalar.activation(sq2[c][:], bank[:], ACT.Square, scale=root_w[:, c : c + 1])
+
+        totals = {}
+
+        def square_and_add(c):
+            bank = second_product(c, h1_q, "bank")
+            sq1 = ring.tile([P, S], F32, name="sq1")
+            if c in SQUARE_ON_VECTOR:
+                plain = ring.tile([P, S], F32, name="plain")
+                nc.vector.tensor_copy(plain[:], bank[:])
+                nc.vector.tensor_tensor(sq1[:], bank[:], plain[:], ALU.mult)
+            else:
+                nc.scalar.activation(sq1[:], bank[:], ACT.Square)
+            total = ring.tile([P, S], F32, name="total")
+            nc.vector.tensor_tensor(total[:], sq1[:], sq2[c][:], ALU.add)
+            totals[c] = total
+
+        def finish(c):
+            result = held([P, S], F32, "result%d" % c)
+            nc.scalar.activation(result[:], totals[c][:], ACT.Sqrt)
+            nc.sync.dma_start(out=out[P * c : P * (c + 1), :], in_=result[:])
+
+        h2_block(0)
+        h2_block(1)
+        gather_stored_words(0, 1)
+        cast_w1(0, 0)
+        gather_stored_scales(0)
+        cast_w1(1, 0)
+        quantize_h(h2_q, "h2", 0)
+        quantize_w1(0, 0)
+        quantize_w1(1, 0)
+        quantize_h(h2_q, "h2", 1)
+        cast_w1(0, 1)
+        h1_block(0)
+        gather_stored_words(0, 0)
+        quantize_w1(0, 1)
+        cast_w1(1, 1)
+        quantize_w1(1, 1)
+        h1_block(1)
+        quantize_h(h1_q, "h1", 0)
+        quantize_h(h1_q, "h1", 1)
+        weighted_square(0)
+        weighted_square(1)
+        weighted_square(2)
+        weighted_square(3)
+        gather_stored_scales(1)
+        gather_stored_words(1, 0)
+        gather_stored_words(1, 1)
+        square_and_add(0)
+        square_and_add(1)
+        square_and_add(2)
+        finish(0)
+        square_and_add(3)
+        finish(1)
+        weighted_square(4)
+        square_and_add(4)
+        finish(2)
+        weighted_square(5)
+        square_and_add(5)
+        finish(3)
+        weighted_square(6)
+        square_and_add(6)
+        finish(4)
+        weighted_square(7)
+        square_and_add(7)
+        finish(5)
+        finish(6)
+        finish(7)

@@ -25,8 +25,8 @@ JC = 128
 HALF = S2 // 2
 CAST_ON_SCALAR = [2]
 SQUARE_ON_VECTOR = []
-WEIGHTED_ON_VECTOR = [4,5,6]
-PLACES = {"w4_w0":0,"v2_w00":0,"w4_s0":2048,"v2_s0":2048,"h2_bf0":4096,"w1_bf01":4096,"h1_bf0":8192,"v2_s1":8192,"v2_w10":8704,"h1_bf1":12288,"v2_w11":12288}
+WEIGHTED_ON_VECTOR = [4,5,6,7]
+PLACES = {"w1_raw00":0,"v2_w00":0,"w1_bf00":8192,"h2_q0_w":8192,"w1_raw01":12288,"h1_bf0":12288,"w1_raw11":20480,"w1_q01_w":20480,"w1_bf11":28672,"v2_w10":28672,"v2_w11":30720,"w1_bf01":32768,"v2_s1":32768,"w4_raw0":36864,"w4_s1":36864}
 
 
 def tile_list_depot_hazard_magnitude_kernel(
@@ -48,7 +48,7 @@ def tile_list_depot_hazard_magnitude_kernel(
         idx2 = keep.tile([P, S2 // 16], U16, name="idx2")
         tab_w = [held([P, T], I32, "tab_w%d" % a) for a in range(PASSES)]
         tab_s = held([P, T], U8, "tab_s")
-        w4_raw = held([P, PASSES, 2 * K], U8, "w4_raw")
+        w4_raw = [held([P, PASSES, K], U8, "w4_raw%d" % b) for b in range(PASSES)]
         w4s_raw = held([P, PASSES, K], U8, "w4s_raw")
         v_s_low = held([P, S], U8, "v_s_low")
         wgt_rows = held([S2 // P, P], F32, "wgt_rows")
@@ -65,22 +65,29 @@ def tile_list_depot_hazard_magnitude_kernel(
         def load_table(a):
             nc.sync.dma_start(out=tab_w[a][:], in_=tab_words[a].rearrange("p t i -> p (t i)").bitcast(I32))
 
+        def load_w4(b):
+            nc.sync.dma_start(
+                out=w4_raw[b][:].bitcast(I32),
+                in_=w4_words[:, :, K * b : K * (b + 1)].rearrange("a p n -> p a n").bitcast(I32),
+            )
+
         nc.sync.dma_start(idx[:], offs)
-        nc.sync.dma_start(out=wgt_rows[:], in_=wgt.rearrange("(c p) -> c p", p=P))
+        nc.scalar.dma_start(out=wgt_rows[:], in_=wgt.rearrange("(c p) -> c p", p=P))
+        nc.sync.dma_start(idx2[:], offs2)
         for q in range(4):
             nc.sync.dma_start(
                 out=tab_s[32 * q : 32 * q + 8, :].bitcast(I32),
                 in_=tab_scales[:, 4 * q : 4 * q + 4, :].bitcast(I32),
             )
-        nc.sync.dma_start(out=w4_raw[:].bitcast(I32), in_=w4_words.rearrange("a p n -> p a n").bitcast(I32))
         load_table(0)
         for q in range(4):
             nc.sync.dma_start(
                 out=w4s_raw[32 * q : 32 * q + 4, :, :].bitcast(I32),
                 in_=w4_scales[:, 4 * q : 4 * q + 4, :].rearrange("a r n -> r a n").bitcast(I32),
             )
+        load_w4(0)
         load_table(1)
-        nc.sync.dma_start(idx2[:], offs2)
+        load_w4(1)
         w1_raw = {}
         for b in range(PASSES):
             for a in range(PASSES):
@@ -115,20 +122,20 @@ def tile_list_depot_hazard_magnitude_kernel(
             w4_w[b] = held([P, PASSES * K], U8, "w4_w%d" % b)
             nc.vector.tensor_copy(
                 w4_w[b][:].bitcast(U16).rearrange("p (a t q) -> p a t q", a=PASSES, t=PACK),
-                w4_raw[:, :, K * b : K * (b + 1)].bitcast(U16).rearrange("p a (q t) -> p a t q", t=PACK),
+                w4_raw[b][:].bitcast(U16).rearrange("p a (q t) -> p a t q", t=PACK),
             )
 
         v_s = held([P, S], U8, "v_s")
         v_w = [held([P, S], U32, "v_w%d" % a) for a in range(PASSES)]
         gather_scales(v_s[:], idx[:])
         nc.scalar.dma_start(out=v_s_low[0 : P - 4, :].bitcast(I32), in_=v_s[4:P, :].bitcast(I32))
-        deal_w4_words(0)
-        deal_w4_words(1)
         gather_words(v_w[0][:], 0, idx[:])
         deal_w4_scales(0)
+        deal_w4_words(0)
         for half in range(2):
             gather_words(v_w[1][:, 256 * half : 256 * (half + 1)], 1, idx[:, 16 * half : 16 * (half + 1)])
         deal_w4_scales(1)
+        deal_w4_words(1)
 
         h_bf = {}
 
@@ -173,8 +180,8 @@ def tile_list_depot_hazard_magnitude_kernel(
 
         def cast_w1(a, b):
             w1_bf[a, b] = held([P, PACK * KP], BF16, "w1_bf%d%d" % (a, b))
-            dst = w1_bf[a, b][:].rearrange("p (t q i) -> p q t i", t=PACK, i=PACK)
-            src = w1_raw[a, b][:].rearrange("p i (q t) -> p q t i", t=PACK)
+            dst = w1_bf[a, b][:].rearrange("p (t q i) -> p q i t", t=PACK, i=PACK)
+            src = w1_raw[a, b][:].rearrange("p i (q t) -> p q i t", t=PACK)
             if PASSES * b + a in CAST_ON_SCALAR:
                 nc.scalar.copy(dst, src)
             else:
@@ -225,81 +232,100 @@ def tile_list_depot_hazard_magnitude_kernel(
                 )
             return bank
 
-        sq2 = {}
+        sq1 = held([P, S2 // P * S], F32, "sq1")
+        sq2 = held([P, S2 // P * S], F32, "sq2")
+        total = held([P, S2 // P * S], F32, "total")
+        result = held([P, S2 // P * S], F32, "result")
 
         def weighted_square(c):
-            bank = second_product(c, h2_q, "bank" if c < 4 else "h_bank")
-            sq2[c] = held([P, S], F32, "sq2_%d" % c)
+            bank = second_product(c, h2_q, "bank" if c < 2 else "h_bank")
+            dst = sq2[:, S * c : S * (c + 1)]
             if c in WEIGHTED_ON_VECTOR:
-                scaled = held([P, S], F32, "scaled%d" % c)
+                scaled = ring.tile([P, S], F32, name="scaled")
                 nc.vector.tensor_scalar(scaled[:], bank[:], root_w[:, c : c + 1], None, ALU.mult)
-                nc.vector.tensor_tensor(sq2[c][:], scaled[:], scaled[:], ALU.mult)
+                nc.vector.scalar_tensor_tensor(dst, bank[:], root_w[:, c : c + 1], scaled[:], ALU.mult, ALU.mult)
             else:
-                nc.scalar.activation(sq2[c][:], bank[:], ACT.Square, scale=root_w[:, c : c + 1])
+                nc.scalar.activation(dst, bank[:], ACT.Square, scale=root_w[:, c : c + 1])
 
-        totals = {}
-
-        def square_and_add(c):
+        def square(c):
             bank = second_product(c, h1_q, "bank")
-            sq1 = ring.tile([P, S], F32, name="sq1")
+            dst = sq1[:, S * c : S * (c + 1)]
             if c in SQUARE_ON_VECTOR:
-                plain = ring.tile([P, S], F32, name="plain")
+                plain = ring.tile([P, S], F32, name="scaled")
                 nc.vector.tensor_copy(plain[:], bank[:])
-                nc.vector.tensor_tensor(sq1[:], bank[:], plain[:], ALU.mult)
+                nc.vector.tensor_tensor(dst, bank[:], plain[:], ALU.mult)
             else:
-                nc.scalar.activation(sq1[:], bank[:], ACT.Square)
-            total = ring.tile([P, S], F32, name="total")
-            nc.vector.tensor_tensor(total[:], sq1[:], sq2[c][:], ALU.add)
-            totals[c] = total
+                nc.scalar.activation(dst, bank[:], ACT.Square)
 
-        def finish(c):
-            result = held([P, S], F32, "result%d" % c)
-            nc.scalar.activation(result[:], totals[c][:], ACT.Sqrt)
-            nc.sync.dma_start(out=out[P * c : P * (c + 1), :], in_=result[:])
+        def add(c, n, engine):
+            cols = slice(S * c, S * (c + n))
+            engine.tensor_tensor(total[:, cols], sq1[:, cols], sq2[:, cols], ALU.add)
+
+        def finish(c, n):
+            cols = slice(S * c, S * (c + n))
+            nc.scalar.activation(result[:, cols], total[:, cols], ACT.Sqrt)
+            nc.sync.dma_start(
+                out=out[P * c : P * (c + n), :].rearrange("(c p) j -> p c j", p=P),
+                in_=result[:, cols].rearrange("p (c j) -> p c j", j=S),
+            )
+
+        def finish_in_halves(c):
+            for k in range(2):
+                cols = slice(S * c + S // 2 * k, S * c + S // 2 * (k + 1))
+                nc.scalar.activation(result[:, cols], total[:, cols], ACT.Sqrt)
+                nc.sync.dma_start(out=out[P * c : P * (c + 1), S // 2 * k : S // 2 * (k + 1)], in_=result[:, cols])
 
         h2_block(0)
         h2_block(1)
+        gather_stored_scales(0)
         gather_stored_words(0, 1)
         cast_w1(0, 0)
-        gather_stored_scales(0)
+        gather_stored_words(0, 0)
+        quantize_w1(0, 0)
         cast_w1(1, 0)
         quantize_h(h2_q, "h2", 0)
-        quantize_w1(0, 0)
         quantize_w1(1, 0)
         quantize_h(h2_q, "h2", 1)
         cast_w1(0, 1)
         h1_block(0)
-        gather_stored_words(0, 0)
-        quantize_w1(0, 1)
         cast_w1(1, 1)
+        quantize_w1(0, 1)
         quantize_w1(1, 1)
         h1_block(1)
+        gather_stored_scales(1)
         quantize_h(h1_q, "h1", 0)
         quantize_h(h1_q, "h1", 1)
         weighted_square(0)
         weighted_square(1)
         weighted_square(2)
         weighted_square(3)
-        gather_stored_scales(1)
         gather_stored_words(1, 0)
         gather_stored_words(1, 1)
-        square_and_add(0)
-        square_and_add(1)
-        square_and_add(2)
-        finish(0)
-        square_and_add(3)
-        finish(1)
         weighted_square(4)
-        square_and_add(4)
-        finish(2)
         weighted_square(5)
-        square_and_add(5)
-        finish(3)
+        square(0)
+        add(0, 1, nc.vector)
+        square(1)
+        add(1, 1, nc.vector)
+        square(2)
+        add(2, 1, nc.vector)
+        finish(0, 1)
+        square(3)
+        add(3, 1, nc.vector)
+        finish(1, 1)
+        square(4)
+        add(4, 1, nc.vector)
+        finish(2, 1)
+        square(5)
+        add(5, 1, nc.vector)
+        finish(3, 1)
         weighted_square(6)
-        square_and_add(6)
-        finish(4)
+        square(6)
+        add(6, 1, nc.vector)
+        finish(4, 1)
         weighted_square(7)
-        square_and_add(7)
-        finish(5)
-        finish(6)
-        finish(7)
+        square(7)
+        add(7, 1, nc.vector)
+        finish(5, 1)
+        finish(6, 1)
+        finish_in_halves(7)

@@ -21,27 +21,73 @@ P = 128
 PACK = 4
 KP = P * PACK
 PASSES = K // KP
-JC = 128
+QUADRANTS = 4
+PLANE_STEP = 4
+MOVED_ROWS = 112
+JC = KP // PACK
 HALF = S2 // 2
-CAST_ON_SCALAR = [2]
-SQUARE_ON_VECTOR = []
-WEIGHTED_ON_VECTOR = [4,5,6,7]
-PLACES = {"w1_raw00":0,"v2_w00":0,"w1_bf00":8192,"h2_q0_w":8192,"w1_raw01":12288,"h1_bf0":12288,"w1_raw11":20480,"w1_q01_w":20480,"w1_bf11":28672,"v2_w10":28672,"v2_w11":30720,"w1_bf01":32768,"v2_s1":32768,"w4_raw0":36864,"w4_s1":36864}
+TILES = S2 // P
+LAST = TILES - 1
+BANKS = 4
+EARLY_TILES = 2
+HALF_TILES = TILES // 2
+FIRST_TILE_ON_VECTOR = 4
+AHEAD = 2
+LAG = 2
+
+FIRST_TENANTS = (
+    ("w4_raw0", PASSES * K),
+    ("w1_raw00", PACK * KP * 4),
+    ("w1_raw10", PACK * KP * 4),
+    ("w1_raw01", PACK * KP * 4),
+    ("w1_raw11", PACK * KP * 4),
+    ("w1_bf01", PACK * KP * 2),
+    ("w1_bf11", PACK * KP * 2),
+)
+SECOND_TENANTS = {
+    "w4_s1": ("w4_raw0", 0),
+    "v2_w00": ("w1_raw00", 0),
+    "h2_q0_w": ("w1_raw10", 0),
+    "h2_q1_w": ("w1_raw10", KP * 4),
+    "h1_bf0": ("w1_raw01", 0),
+    "w1_q01_w": ("w1_raw11", 0),
+    "v2_s1": ("w1_bf01", 0),
+    "v2_w10": ("w1_bf11", 0),
+    "v2_w11": ("w1_bf11", HALF * 4),
+}
+
+
+def shared_offsets():
+    offsets = {}
+    start = 0
+    for name, size in FIRST_TENANTS:
+        offsets[name] = start
+        start = start + size
+    for name, (first, within) in SECOND_TENANTS.items():
+        offsets[name] = offsets[first] + within
+    return offsets
 
 
 def tile_list_depot_hazard_magnitude_kernel(
     tc, tab_words, tab_scales, offs, offs2, w1, w4_words, w4_scales, wgt, out
 ):
     nc = tc.nc
+    offsets = shared_offsets()
     with ExitStack() as ctx:
         keep = ctx.enter_context(tc.tile_pool(name="keep", bufs=1))
-        stage = ctx.enter_context(tc.tile_pool(name="stage", bufs=1))
+        shared = ctx.enter_context(tc.tile_pool(name="shared", bufs=1))
         ring = ctx.enter_context(tc.tile_pool(name="ring", bufs=4))
-        psum = ctx.enter_context(tc.psum_pool(name="psum", bufs=4))
+        psum = ctx.enter_context(tc.psum_pool(name="psum", bufs=1))
+
+        def h_bank(n):
+            return psum.tile([P, KP], F32, name="h_bank%d" % (n % BANKS))
+
+        def e_bank(n):
+            return psum.tile([P, KP], F32, name="e_bank%d" % (n % BANKS))
 
         def held(shape, dtype, name):
-            if name in PLACES:
-                return stage.tile(shape, dtype, name=name, align_bytes=64, offset=PLACES[name])
+            if name in offsets:
+                return shared.tile(shape, dtype, name=name, align_bytes=64, offset=offsets[name])
             return keep.tile(shape, dtype, name=name, align_bytes=64)
 
         idx = keep.tile([P, S // 16], U16, name="idx")
@@ -51,10 +97,10 @@ def tile_list_depot_hazard_magnitude_kernel(
         w4_raw = [held([P, PASSES, K], U8, "w4_raw%d" % b) for b in range(PASSES)]
         w4s_raw = held([P, PASSES, K], U8, "w4s_raw")
         v_s_low = held([P, S], U8, "v_s_low")
-        wgt_rows = held([S2 // P, P], F32, "wgt_rows")
+        wgt_rows = held([TILES, P], F32, "wgt_rows")
         root_rows = held([P, P], F32, "root_rows")
         ident = held([P, P], F32, "ident")
-        root_w = held([P, S2 // P], F32, "root_w")
+        root_w = held([P, TILES], F32, "root_w")
 
         nc.gpsimd.memset(tab_s[:].bitcast(I32), 0)
         make_identity(nc, ident[:])
@@ -74,16 +120,16 @@ def tile_list_depot_hazard_magnitude_kernel(
         nc.sync.dma_start(idx[:], offs)
         nc.scalar.dma_start(out=wgt_rows[:], in_=wgt.rearrange("(c p) -> c p", p=P))
         nc.sync.dma_start(idx2[:], offs2)
-        for q in range(4):
+        for g in range(QUADRANTS):
             nc.sync.dma_start(
-                out=tab_s[32 * q : 32 * q + 8, :].bitcast(I32),
-                in_=tab_scales[:, 4 * q : 4 * q + 4, :].bitcast(I32),
+                out=tab_s[32 * g : 32 * g + PASSES * PLANE_STEP, :].bitcast(I32),
+                in_=tab_scales[:, 4 * g : 4 * g + 4, :].bitcast(I32),
             )
         load_table(0)
-        for q in range(4):
+        for g in range(QUADRANTS):
             nc.sync.dma_start(
-                out=w4s_raw[32 * q : 32 * q + 4, :, :].bitcast(I32),
-                in_=w4_scales[:, 4 * q : 4 * q + 4, :].rearrange("a r n -> r a n").bitcast(I32),
+                out=w4s_raw[32 * g : 32 * g + 4, :, :].bitcast(I32),
+                in_=w4_scales[:, 4 * g : 4 * g + 4, :].rearrange("a r n -> r a n").bitcast(I32),
             )
         load_w4(0)
         load_table(1)
@@ -97,16 +143,16 @@ def tile_list_depot_hazard_magnitude_kernel(
                     in_=w1[KP * a : KP * (a + 1), KP * b : KP * (b + 1)].rearrange("(p i) c -> p i c", i=PACK),
                 )
 
-        nc.scalar.activation(root_rows[0 : S2 // P, :], wgt_rows[:], ACT.Sqrt)
-        root_cols = psum.tile([P, KP], F32, name="bank")
+        nc.scalar.activation(root_rows[0:TILES, :], wgt_rows[:], ACT.Sqrt)
+        root_cols = e_bank(0)
         nc.tensor.transpose(root_cols[:, 0:P], root_rows[:], ident[:])
-        nc.scalar.copy(root_w[:], root_cols[:, 0 : S2 // P])
+        nc.scalar.copy(root_w[:], root_cols[:, 0:TILES])
 
-        def gather_words(dst, a, offsets):
-            nc.vector.tensor_copy(dst, tab_w[a][:].bitcast(U32).indirect(offsets))
+        def gather_words(dst, a, entries):
+            nc.vector.tensor_copy(dst, tab_w[a][:].bitcast(U32).indirect(entries))
 
-        def gather_scales(dst, offsets):
-            nc.vector.tensor_copy(dst, tab_s[:].indirect(offsets))
+        def gather_scales(dst, entries):
+            nc.vector.tensor_copy(dst, tab_s[:].indirect(entries))
 
         w4_w = {}
         w4_s = {}
@@ -128,12 +174,17 @@ def tile_list_depot_hazard_magnitude_kernel(
         v_s = held([P, S], U8, "v_s")
         v_w = [held([P, S], U32, "v_w%d" % a) for a in range(PASSES)]
         gather_scales(v_s[:], idx[:])
-        nc.scalar.dma_start(out=v_s_low[0 : P - 4, :].bitcast(I32), in_=v_s[4:P, :].bitcast(I32))
+        nc.scalar.dma_start(
+            out=v_s_low[0:MOVED_ROWS, :].bitcast(I32),
+            in_=v_s[PLANE_STEP : PLANE_STEP + MOVED_ROWS, :].bitcast(I32),
+        )
         gather_words(v_w[0][:], 0, idx[:])
         deal_w4_scales(0)
         deal_w4_words(0)
         for half in range(2):
-            gather_words(v_w[1][:, 256 * half : 256 * (half + 1)], 1, idx[:, 16 * half : 16 * (half + 1)])
+            gather_words(
+                v_w[1][:, S // 2 * half : S // 2 * (half + 1)], 1, idx[:, S // 32 * half : S // 32 * (half + 1)]
+            )
         deal_w4_scales(1)
         deal_w4_words(1)
 
@@ -143,7 +194,7 @@ def tile_list_depot_hazard_magnitude_kernel(
             h_bf[name, b] = held([P, PACK * S], BF16, "%s_bf%d" % (name, b))
             for jc in range(S // JC):
                 cols = slice(JC * jc, JC * (jc + 1))
-                bank = psum.tile([P, KP], F32, name="h_bank")
+                bank = h_bank(jc)
                 for a in range(PASSES):
                     for t in range(PACK):
                         codes, scales = stationary(a, t)
@@ -178,14 +229,12 @@ def tile_list_depot_hazard_magnitude_kernel(
         w1_bf = {}
         w1_q = {}
 
-        def cast_w1(a, b):
+        def cast_w1(a, b, copy):
             w1_bf[a, b] = held([P, PACK * KP], BF16, "w1_bf%d%d" % (a, b))
-            dst = w1_bf[a, b][:].rearrange("p (t q i) -> p q i t", t=PACK, i=PACK)
-            src = w1_raw[a, b][:].rearrange("p i (q t) -> p q i t", t=PACK)
-            if PASSES * b + a in CAST_ON_SCALAR:
-                nc.scalar.copy(dst, src)
-            else:
-                nc.vector.tensor_copy(dst, src)
+            copy(
+                w1_bf[a, b][:].rearrange("p (t q i) -> p q i t", t=PACK, i=PACK),
+                w1_raw[a, b][:].rearrange("p i (q t) -> p q i t", t=PACK),
+            )
 
         def quantize_w1(a, b):
             w1_q[a, b] = quantize("w1_q%d%d" % (a, b), w1_bf[a, b])
@@ -195,137 +244,109 @@ def tile_list_depot_hazard_magnitude_kernel(
                 codes, scales = w1_q[a, b]
                 return codes[:, P * t : P * (t + 1)].bitcast(FP8X4), scales[:, P * t : P * (t + 1)]
 
-            first_products("h1", b, stationary, [v_s[:], v_s[4:P, :]])
+            first_products("h1", b, stationary, [v_s[:], v_s[PLANE_STEP:P, :]])
 
-        h1_q = {}
-        h2_q = {}
+        h_q = {}
 
-        def quantize_h(store, name, b):
-            store[b] = quantize("%s_q%d" % (name, b), h_bf[name, b])
+        def quantize_h(name, b):
+            h_q[name, b] = quantize("%s_q%d" % (name, b), h_bf[name, b])
 
         v2_w = {}
         v2_s = {}
 
-        def stored_offsets(half):
+        def stored_entries(half):
             return idx2[:, HALF // 16 * half : HALF // 16 * (half + 1)]
 
         def gather_stored_scales(half):
             v2_s[half] = held([P, HALF], U8, "v2_s%d" % half)
-            gather_scales(v2_s[half][:], stored_offsets(half))
+            gather_scales(v2_s[half][:], stored_entries(half))
 
         def gather_stored_words(half, b):
             v2_w[half, b] = held([P, HALF], U32, "v2_w%d%d" % (half, b))
-            gather_words(v2_w[half, b][:], b, stored_offsets(half))
+            gather_words(v2_w[half, b][:], b, stored_entries(half))
 
-        def second_product(c, h_q, bank_name):
-            half, cols = divmod(P * c, HALF)
-            bank = psum.tile([P, S], F32, name=bank_name)
+        def second_product(c, name, bank):
+            half, first = divmod(P * c, HALF)
             for b in range(PASSES):
+                codes, scales = h_q[name, b]
                 nc.tensor.matmul_mx(
                     out=bank[:],
-                    lhsT=v2_w[half, b][:, cols : cols + P].bitcast(FP8X4),
-                    lhsT_scale=v2_s[half][4 * b : P, cols : cols + P],
-                    rhs=h_q[b][0][:].bitcast(FP8X4),
-                    rhs_scale=h_q[b][1][:],
+                    lhsT=v2_w[half, b][:, first : first + P].bitcast(FP8X4),
+                    lhsT_scale=v2_s[half][PLANE_STEP * b : P, first : first + P],
+                    rhs=codes[:].bitcast(FP8X4),
+                    rhs_scale=scales[:],
                     start=(b == 0),
                     stop=(b == PASSES - 1),
                 )
-            return bank
 
-        sq1 = held([P, S2 // P * S], F32, "sq1")
-        sq2 = held([P, S2 // P * S], F32, "sq2")
-        total = held([P, S2 // P * S], F32, "total")
-        result = held([P, S2 // P * S], F32, "result")
+        sq1 = held([P, TILES * S], F32, "sq1")
+        sq2 = held([P, TILES * S], F32, "sq2")
+        total = held([P, TILES * S], F32, "total")
+        result = held([P, TILES * S], F32, "result")
 
         def weighted_square(c):
-            bank = second_product(c, h2_q, "bank" if c < 2 else "h_bank")
+            bank = e_bank(1 + c) if c < EARLY_TILES else h_bank(c - EARLY_TILES)
+            second_product(c, "h2", bank)
             dst = sq2[:, S * c : S * (c + 1)]
-            if c in WEIGHTED_ON_VECTOR:
+            root = root_w[:, c : c + 1]
+            if c >= FIRST_TILE_ON_VECTOR:
                 scaled = ring.tile([P, S], F32, name="scaled")
-                nc.vector.tensor_scalar(scaled[:], bank[:], root_w[:, c : c + 1], None, ALU.mult)
-                nc.vector.scalar_tensor_tensor(dst, bank[:], root_w[:, c : c + 1], scaled[:], ALU.mult, ALU.mult)
+                nc.vector.tensor_scalar(scaled[:], bank[:], root, None, ALU.mult)
+                nc.vector.tensor_tensor(dst, scaled[:], scaled[:], ALU.mult)
             else:
-                nc.scalar.activation(dst, bank[:], ACT.Square, scale=root_w[:, c : c + 1])
+                nc.scalar.activation(dst, bank[:], ACT.Square, scale=root)
 
         def square(c):
-            bank = second_product(c, h1_q, "bank")
-            dst = sq1[:, S * c : S * (c + 1)]
-            if c in SQUARE_ON_VECTOR:
-                plain = ring.tile([P, S], F32, name="scaled")
-                nc.vector.tensor_copy(plain[:], bank[:])
-                nc.vector.tensor_tensor(dst, bank[:], plain[:], ALU.mult)
-            else:
-                nc.scalar.activation(dst, bank[:], ACT.Square)
+            bank = e_bank(1 + EARLY_TILES + c)
+            second_product(c, "h1", bank)
+            nc.scalar.activation(sq1[:, S * c : S * (c + 1)], bank[:], ACT.Square)
 
-        def add(c, n, engine):
-            cols = slice(S * c, S * (c + n))
-            engine.tensor_tensor(total[:, cols], sq1[:, cols], sq2[:, cols], ALU.add)
+        def add(c, first, width):
+            cols = slice(S * c + first, S * c + first + width)
+            nc.vector.tensor_tensor(total[:, cols], sq1[:, cols], sq2[:, cols], ALU.add)
 
-        def finish(c, n):
-            cols = slice(S * c, S * (c + n))
+        def root_and_store(c, first, width):
+            cols = slice(S * c + first, S * c + first + width)
             nc.scalar.activation(result[:, cols], total[:, cols], ACT.Sqrt)
-            nc.sync.dma_start(
-                out=out[P * c : P * (c + n), :].rearrange("(c p) j -> p c j", p=P),
-                in_=result[:, cols].rearrange("p (c j) -> p c j", j=S),
-            )
-
-        def finish_in_halves(c):
-            for k in range(2):
-                cols = slice(S * c + S // 2 * k, S * c + S // 2 * (k + 1))
-                nc.scalar.activation(result[:, cols], total[:, cols], ACT.Sqrt)
-                nc.sync.dma_start(out=out[P * c : P * (c + 1), S // 2 * k : S // 2 * (k + 1)], in_=result[:, cols])
+            nc.sync.dma_start(out=out[P * c : P * (c + 1), first : first + width], in_=result[:, cols])
 
         h2_block(0)
         h2_block(1)
         gather_stored_scales(0)
         gather_stored_words(0, 1)
-        cast_w1(0, 0)
+        cast_w1(0, 0, nc.vector.tensor_copy)
         gather_stored_words(0, 0)
         quantize_w1(0, 0)
-        cast_w1(1, 0)
-        quantize_h(h2_q, "h2", 0)
+        cast_w1(1, 0, nc.vector.tensor_copy)
         quantize_w1(1, 0)
-        quantize_h(h2_q, "h2", 1)
-        cast_w1(0, 1)
+        quantize_h("h2", 0)
+        quantize_h("h2", 1)
+        cast_w1(0, 1, nc.scalar.copy)
         h1_block(0)
-        cast_w1(1, 1)
+        cast_w1(1, 1, nc.vector.tensor_copy)
         quantize_w1(0, 1)
         quantize_w1(1, 1)
         h1_block(1)
         gather_stored_scales(1)
-        quantize_h(h1_q, "h1", 0)
-        quantize_h(h1_q, "h1", 1)
-        weighted_square(0)
-        weighted_square(1)
-        weighted_square(2)
-        weighted_square(3)
+        quantize_h("h1", 0)
+        quantize_h("h1", 1)
+        for c in range(HALF_TILES):
+            weighted_square(c)
         gather_stored_words(1, 0)
         gather_stored_words(1, 1)
-        weighted_square(4)
-        weighted_square(5)
-        square(0)
-        add(0, 1, nc.vector)
-        square(1)
-        add(1, 1, nc.vector)
-        square(2)
-        add(2, 1, nc.vector)
-        finish(0, 1)
-        square(3)
-        add(3, 1, nc.vector)
-        finish(1, 1)
-        square(4)
-        add(4, 1, nc.vector)
-        finish(2, 1)
-        square(5)
-        add(5, 1, nc.vector)
-        finish(3, 1)
-        weighted_square(6)
-        square(6)
-        add(6, 1, nc.vector)
-        finish(4, 1)
-        weighted_square(7)
-        square(7)
-        add(7, 1, nc.vector)
-        finish(5, 1)
-        finish(6, 1)
-        finish_in_halves(7)
+
+        for c in range(HALF_TILES, HALF_TILES + 2):
+            weighted_square(c)
+        for c in range(TILES):
+            square(c)
+            if c < LAST:
+                add(c, 0, S)
+            if HALF_TILES + 2 <= c + AHEAD < TILES:
+                weighted_square(c + AHEAD)
+            if c >= LAG:
+                root_and_store(c - LAG, 0, S)
+        for c in range(TILES - LAG, LAST):
+            root_and_store(c, 0, S)
+        for first in (0, S // 2):
+            add(LAST, first, S // 2)
+            root_and_store(LAST, first, S // 2)

@@ -30,8 +30,8 @@ TILES = S2 // P
 LAST = TILES - 1
 BANKS = 4
 EARLY_TILES = 2
-HALF_TILES = TILES // 2
-FIRST_TILE_ON_VECTOR = 4
+HALF_TILES = HALF // P
+FIRST_TILE_ON_VECTOR = 5
 AHEAD = 2
 LAG = 2
 
@@ -43,6 +43,7 @@ FIRST_TENANTS = (
     ("w1_raw11", PACK * KP * 4),
     ("w1_bf01", PACK * KP * 2),
     ("w1_bf11", PACK * KP * 2),
+    ("h1_bf1", PACK * S * 2),
 )
 SECOND_TENANTS = {
     "w4_s1": ("w4_raw0", 0),
@@ -53,7 +54,7 @@ SECOND_TENANTS = {
     "w1_q01_w": ("w1_raw11", 0),
     "v2_s1": ("w1_bf01", 0),
     "v2_w10": ("w1_bf11", 0),
-    "v2_w11": ("w1_bf11", HALF * 4),
+    "v2_w11": ("h1_bf1", 0),
 }
 
 
@@ -335,13 +336,11 @@ def tile_list_depot_hazard_magnitude_kernel(
         gather_stored_words(1, 0)
         gather_stored_words(1, 1)
 
-        for c in range(HALF_TILES, HALF_TILES + 2):
-            weighted_square(c)
         for c in range(TILES):
             square(c)
             if c < LAST:
                 add(c, 0, S)
-            if HALF_TILES + 2 <= c + AHEAD < TILES:
+            if HALF_TILES <= c + AHEAD < TILES:
                 weighted_square(c + AHEAD)
             if c >= LAG:
                 root_and_store(c - LAG, 0, S)

from contextlib import ExitStack

import concourse.mybir as mybir
from concourse.masks import make_identity

K, T, S, S2 = 1024, 2048, 512, 1024
FLOPS = 2 * (2 * K * K * S + 2 * K * S2 * S)

F32 = mybir.dt.float32
BF16 = mybir.dt.bfloat16
I32 = mybir.dt.int32
U32 = mybir.dt.uint32
U16 = mybir.dt.uint16
U8 = mybir.dt.uint8
FP8X4 = mybir.dt.float8_e4m3fn_x4
FP4X4 = mybir.dt.float4_e2m1fn_x4
ACT = mybir.ActivationFunctionType
ALU = mybir.AluOpType

P = 128
PACK = 4
KP = P * PACK
PASSES = K // KP
QUADRANTS = 4
PLANE_STEP = 4
MOVED_ROWS = 112
JC = KP // PACK
HALF = S2 // 2
TILES = S2 // P
LAST = TILES - 1
BANKS = 4
EARLY_TILES = 2
HALF_TILES = HALF // P
FIRST_TILE_ON_VECTOR = 5
AHEAD = 2
LAG = 2

FIRST_TENANTS = (
    ("w4_raw0", PASSES * K),
    ("w1_raw00", PACK * KP * 4),
    ("w1_raw10", PACK * KP * 4),
    ("w1_raw01", PACK * KP * 4),
    ("w1_raw11", PACK * KP * 4),
    ("w1_bf01", PACK * KP * 2),
    ("w1_bf11", PACK * KP * 2),
    ("h1_bf1", PACK * S * 2),
)
SECOND_TENANTS = {
    "w4_s1": ("w4_raw0", 0),
    "v2_w00": ("w1_raw00", 0),
    "h2_q0_w": ("w1_raw10", 0),
    "h2_q1_w": ("w1_raw10", KP * 4),
    "h1_bf0": ("w1_raw01", 0),
    "w1_q01_w": ("w1_raw11", 0),
    "v2_s1": ("w1_bf01", 0),
    "v2_w10": ("w1_bf11", 0),
    "v2_w11": ("h1_bf1", 0),
}


def shared_offsets():
    offsets = {}
    start = 0
    for name, size in FIRST_TENANTS:
        offsets[name] = start
        start = start + size
    for name, (first, within) in SECOND_TENANTS.items():
        offsets[name] = offsets[first] + within
    return offsets


def tile_list_depot_hazard_magnitude_kernel(
    tc, tab_words, tab_scales, offs, offs2, w1, w4_words, w4_scales, wgt, out
):
    nc = tc.nc
    offsets = shared_offsets()
    with ExitStack() as ctx:
        keep = ctx.enter_context(tc.tile_pool(name="keep", bufs=1))
        shared = ctx.enter_context(tc.tile_pool(name="shared", bufs=1))
        ring = ctx.enter_context(tc.tile_pool(name="ring", bufs=4))
        psum = ctx.enter_context(tc.psum_pool(name="psum", bufs=1))

        def h_bank(n):
            return psum.tile([P, KP], F32, name="h_bank%d" % (n % BANKS))

        def e_bank(n):
            return psum.tile([P, KP], F32, name="e_bank%d" % (n % BANKS))

        def held(shape, dtype, name):
            if name in offsets:
                return shared.tile(shape, dtype, name=name, align_bytes=64, offset=offsets[name])
            return keep.tile(shape, dtype, name=name, align_bytes=64)

        idx = keep.tile([P, S // 16], U16, name="idx")
        idx2 = keep.tile([P, S2 // 16], U16, name="idx2")
        tab_w = [held([P, T], I32, "tab_w%d" % a) for a in range(PASSES)]
        tab_s = held([P, T], U8, "tab_s")
        w4_raw = [held([P, PASSES, K], U8, "w4_raw%d" % b) for b in range(PASSES)]
        w4s_raw = held([P, PASSES, K], U8, "w4s_raw")
        v_s_low = held([P, S], U8, "v_s_low")
        wgt_rows = held([TILES, P], F32, "wgt_rows")
        root_rows = held([P, P], F32, "root_rows")
        ident = held([P, P], F32, "ident")
        root_w = held([P, TILES], F32, "root_w")

        nc.gpsimd.memset(tab_s[:].bitcast(I32), 0)
        make_identity(nc, ident[:])
        nc.vector.memset(w4s_raw[:].rearrange("p a n -> p (a n)").bitcast(I32), 0)
        nc.vector.memset(root_rows[:], 0.0)
        nc.vector.memset(v_s_low[:].bitcast(I32), 0)

        def load_table(a):
            nc.sync.dma_start(out=tab_w[a][:], in_=tab_words[a].rearrange("p t i -> p (t i)").bitcast(I32))

        def load_w4(b):
            nc.sync.dma_start(
                out=w4_raw[b][:].bitcast(I32),
                in_=w4_words[:, :, K * b : K * (b + 1)].rearrange("a p n -> p a n").bitcast(I32),
            )

        nc.sync.dma_start(idx[:], offs)
        nc.scalar.dma_start(out=wgt_rows[:], in_=wgt.rearrange("(c p) -> c p", p=P))
        nc.sync.dma_start(idx2[:], offs2)
        for g in range(QUADRANTS):
            nc.sync.dma_start(
                out=tab_s[32 * g : 32 * g + PASSES * PLANE_STEP, :].bitcast(I32),
                in_=tab_scales[:, 4 * g : 4 * g + 4, :].bitcast(I32),
            )
        load_table(0)
        for g in range(QUADRANTS):
            nc.sync.dma_start(
                out=w4s_raw[32 * g : 32 * g + 4, :, :].bitcast(I32),
                in_=w4_scales[:, 4 * g : 4 * g + 4, :].rearrange("a r n -> r a n").bitcast(I32),
            )
        load_w4(0)
        load_table(1)
        load_w4(1)
        w1_raw = {}
        for b in range(PASSES):
            for a in range(PASSES):
                w1_raw[a, b] = held([P, PACK, KP], F32, "w1_raw%d%d" % (a, b))
                nc.sync.dma_start(
                    out=w1_raw[a, b][:],
                    in_=w1[KP * a : KP * (a + 1), KP * b : KP * (b + 1)].rearrange("(p i) c -> p i c", i=PACK),
                )

        nc.scalar.activation(root_rows[0:TILES, :], wgt_rows[:], ACT.Sqrt)
        root_cols = e_bank(0)
        nc.tensor.transpose(root_cols[:, 0:P], root_rows[:], ident[:])
        nc.scalar.copy(root_w[:], root_cols[:, 0:TILES])

        def gather_words(dst, a, entries):
            nc.vector.tensor_copy(dst, tab_w[a][:].bitcast(U32).indirect(entries))

        def gather_scales(dst, entries):
            nc.vector.tensor_copy(dst, tab_s[:].indirect(entries))

        w4_w = {}
        w4_s = {}

        def deal_w4_scales(b):
            w4_s[b] = held([P, PASSES * KP], U8, "w4_s%d" % b)
            nc.vector.tensor_copy(
                w4_s[b][:].rearrange("p (a t q) -> p a t q", a=PASSES, t=PACK),
                w4s_raw[:, :, KP * b : KP * (b + 1)].rearrange("p a (q t) -> p a t q", t=PACK),
            )

        def deal_w4_words(b):
            w4_w[b] = held([P, PASSES * K], U8, "w4_w%d" % b)
            nc.vector.tensor_copy(
                w4_w[b][:].bitcast(U16).rearrange("p (a t q) -> p a t q", a=PASSES, t=PACK),
                w4_raw[b][:].bitcast(U16).rearrange("p a (q t) -> p a t q", t=PACK),
            )

        v_s = held([P, S], U8, "v_s")
        v_w = [held([P, S], U32, "v_w%d" % a) for a in range(PASSES)]
        gather_scales(v_s[:], idx[:])
        nc.scalar.dma_start(
            out=v_s_low[0:MOVED_ROWS, :].bitcast(I32),
            in_=v_s[PLANE_STEP : PLANE_STEP + MOVED_ROWS, :].bitcast(I32),
        )
        gather_words(v_w[0][:], 0, idx[:])
        deal_w4_scales(0)
        deal_w4_words(0)
        for half in range(2):
            gather_words(
                v_w[1][:, S // 2 * half : S // 2 * (half + 1)], 1, idx[:, S // 32 * half : S // 32 * (half + 1)]
            )
        deal_w4_scales(1)
        deal_w4_words(1)

        h_bf = {}

        def first_products(name, b, stationary, v_scales):
            h_bf[name, b] = held([P, PACK * S], BF16, "%s_bf%d" % (name, b))
            for jc in range(S // JC):
                cols = slice(JC * jc, JC * (jc + 1))
                bank = h_bank(jc)
                for a in range(PASSES):
                    for t in range(PACK):
                        codes, scales = stationary(a, t)
                        nc.tensor.matmul_mx(
                            out=bank[:, JC * t : JC * (t + 1)],
                            lhsT=codes,
                            lhsT_scale=scales,
                            rhs=v_w[a][:, cols].bitcast(FP8X4),
                            rhs_scale=v_scales[a][:, cols],
                            start=(a == 0 and t == 0),
                            stop=(a == PASSES - 1 and t == PACK - 1),
                        )
                nc.scalar.activation(
                    h_bf[name, b][:, KP * jc : KP * (jc + 1)].rearrange("p (j t) -> p j t", t=PACK),
                    bank[:].rearrange("p (t j) -> p j t", t=PACK),
                    ACT.Abs,
                )

        def quantize(name, values):
            codes = held([P, KP], U32, name + "_w")
            scales = held([P, KP], U8, name + "_s")
            nc.vector.quantize_mx(out=codes[:].bitcast(FP8X4), scales=scales[:], in_=values[:])
            return codes, scales

        def h2_block(b):
            def stationary(a, t):
                c = P * (PACK * a + t)
                return w4_w[b][:, 2 * c : 2 * (c + P)].bitcast(FP4X4), w4_s[b][:, c : c + P]

            first_products("h2", b, stationary, [v_s[:], v_s_low[:]])

        w1_bf = {}
        w1_q = {}

        def cast_w1(a, b, copy):
            w1_bf[a, b] = held([P, PACK * KP], BF16, "w1_bf%d%d" % (a, b))
            copy(
                w1_bf[a, b][:].rearrange("p (t q i) -> p q i t", t=PACK, i=PACK),
                w1_raw[a, b][:].rearrange("p i (q t) -> p q i t", t=PACK),
            )

        def quantize_w1(a, b):
            w1_q[a, b] = quantize("w1_q%d%d" % (a, b), w1_bf[a, b])

        def h1_block(b):
            def stationary(a, t):
                codes, scales = w1_q[a, b]
                return codes[:, P * t : P * (t + 1)].bitcast(FP8X4), scales[:, P * t : P * (t + 1)]

            first_products("h1", b, stationary, [v_s[:], v_s[PLANE_STEP:P, :]])

        h_q = {}

        def quantize_h(name, b):
            h_q[name, b] = quantize("%s_q%d" % (name, b), h_bf[name, b])

        v2_w = {}
        v2_s = {}

        def stored_entries(half):
            return idx2[:, HALF // 16 * half : HALF // 16 * (half + 1)]

        def gather_stored_scales(half):
            v2_s[half] = held([P, HALF], U8, "v2_s%d" % half)
            gather_scales(v2_s[half][:], stored_entries(half))

        def gather_stored_words(half, b):
            v2_w[half, b] = held([P, HALF], U32, "v2_w%d%d" % (half, b))
            gather_words(v2_w[half, b][:], b, stored_entries(half))

        def second_product(c, name, bank):
            half, first = divmod(P * c, HALF)
            for b in range(PASSES):
                codes, scales = h_q[name, b]
                nc.tensor.matmul_mx(
                    out=bank[:],
                    lhsT=v2_w[half, b][:, first : first + P].bitcast(FP8X4),
                    lhsT_scale=v2_s[half][PLANE_STEP * b : P, first : first + P],
                    rhs=codes[:].bitcast(FP8X4),
                    rhs_scale=scales[:],
                    start=(b == 0),
                    stop=(b == PASSES - 1),
                )

        sq1 = held([P, TILES * S], F32, "sq1")
        sq2 = held([P, TILES * S], F32, "sq2")
        total = held([P, TILES * S], F32, "total")
        result = held([P, TILES * S], F32, "result")

        def weighted_square(c):
            bank = e_bank(1 + c) if c < EARLY_TILES else h_bank(c - EARLY_TILES)
            second_product(c, "h2", bank)
            dst = sq2[:, S * c : S * (c + 1)]
            root = root_w[:, c : c + 1]
            if c >= FIRST_TILE_ON_VECTOR:
                scaled = ring.tile([P, S], F32, name="scaled")
                nc.vector.tensor_scalar(scaled[:], bank[:], root, None, ALU.mult)
                nc.vector.tensor_tensor(dst, scaled[:], scaled[:], ALU.mult)
            else:
                nc.scalar.activation(dst, bank[:], ACT.Square, scale=root)

        def square(c):
            bank = e_bank(1 + EARLY_TILES + c)
            second_product(c, "h1", bank)
            nc.scalar.activation(sq1[:, S * c : S * (c + 1)], bank[:], ACT.Square)

        def add(c, first, width):
            cols = slice(S * c + first, S * c + first + width)
            nc.vector.tensor_tensor(total[:, cols], sq1[:, cols], sq2[:, cols], ALU.add)

        def root_and_store(c, first, width):
            cols = slice(S * c + first, S * c + first + width)
            nc.scalar.activation(result[:, cols], total[:, cols], ACT.Sqrt)
            nc.sync.dma_start(out=out[P * c : P * (c + 1), first : first + width], in_=result[:, cols])

        h2_block(0)
        h2_block(1)
        gather_stored_scales(0)
        gather_stored_words(0, 1)
        cast_w1(0, 0, nc.vector.tensor_copy)
        gather_stored_words(0, 0)
        quantize_w1(0, 0)
        cast_w1(1, 0, nc.vector.tensor_copy)
        quantize_w1(1, 0)
        quantize_h("h2", 0)
        quantize_h("h2", 1)
        cast_w1(0, 1, nc.scalar.copy)
        h1_block(0)
        cast_w1(1, 1, nc.vector.tensor_copy)
        quantize_w1(0, 1)
        quantize_w1(1, 1)
        h1_block(1)
        gather_stored_scales(1)
        quantize_h("h1", 0)
        quantize_h("h1", 1)
        for c in range(HALF_TILES):
            weighted_square(c)
        gather_stored_words(1, 0)
        gather_stored_words(1, 1)

        for c in range(TILES):
            square(c)
            if c < LAST:
                add(c, 0, S)
            if HALF_TILES <= c + AHEAD < TILES:
                weighted_square(c + AHEAD)
            if c >= LAG:
                root_and_store(c - LAG, 0, S)
        for c in range(TILES - LAG, LAST):
            root_and_store(c, 0, S)
        for first in (0, S // 2):
            add(LAST, first, S // 2)
            root_and_store(LAST, first, S // 2)
